import numpy as np
import ml_dtypes


def mxq(x, axis, fmt="e4m3"):
    dtype, down = {"e4m3": (ml_dtypes.float8_e4m3fn, 7), "e5m2": (ml_dtypes.float8_e5m2, 14)}[fmt]
    v = np.moveaxis(np.asarray(x, np.float32).astype(ml_dtypes.bfloat16).astype(np.float64), axis, -1)
    blocks = v.reshape(v.shape[:-1] + (-1, 32))
    amax = np.abs(blocks).max(-1, keepdims=True)
    byte = np.maximum(np.where(amax > 0, np.frexp(amax)[1] - 1 + 127, 0) - down, 1)
    scale = np.exp2(byte - 127.0)
    codes = (blocks / scale).astype(np.float32).astype(dtype).astype(np.float64)
    return np.moveaxis((codes * scale).reshape(v.shape), -1, axis)


WIDE = False


def mx_kscale(k):
    if not WIDE:
        return np.ones(k)
    levels = np.array([10, -10, 5, -5, 0])
    if k % 512:
        return np.exp2(np.random.permutation(np.resize(levels, k // 32))).repeat(32)
    a = np.empty((k // 512, 16))
    for p in range(k // 512):
        a[p, :8] = np.random.permutation(np.resize(levels, 8))
        for g in range(8):
            far = levels[np.abs(levels - a[p, g]) >= 10]
            a[p, g + 8] = far[np.random.randint(len(far))]
    return np.exp2(a.ravel()).repeat(32)


BF16 = ml_dtypes.bfloat16


def bf(x):
    return np.asarray(x, np.float32).astype(BF16)


def f64(x):
    return np.asarray(x).astype(np.float64)


E2M1 = np.array([0.0, 0.5, 1.0, 1.5, 2.0, 3.0, 4.0, 6.0, -0.0, -0.5, -1.0, -1.5, -2.0, -3.0, -4.0, -6.0])


def pack_weight(w, fmt):
    k, n = w.shape
    w = f64(bf(w)).reshape(k // 32, 32, n)
    amax = np.abs(w).max(1)
    if fmt == "e4m3":
        byte = np.frexp(amax)[1] - 1 + 127 - 7
    else:
        mant, ex = np.frexp(amax / 6.0)
        byte = np.where(mant > 0.5, ex, ex - 1) + 127
    byte = np.clip(np.where(amax > 0, byte, 1), 1, 254)
    scaled = (w * np.exp2(127.0 - byte)[:, None, :]).reshape(k, n).astype(np.float32)
    by_word = np.ascontiguousarray(scaled.reshape(k // 512, 128, 4, n).transpose(0, 1, 3, 2))
    if fmt == "e4m3":
        words = by_word.astype(ml_dtypes.float8_e4m3fn).view(np.uint8)
    else:
        c = by_word.astype(ml_dtypes.float4_e2m1fn).view(np.uint8) & 0xF
        words = c[..., 0::2] | (c[..., 1::2] << 4)
    return np.ascontiguousarray(words), np.ascontiguousarray(byte.astype(np.uint8).reshape(k // 512, 16, n))


def unpack_weight(words, scales, fmt):
    g, p, n, _ = words.shape
    if fmt == "e4m3":
        vals = np.ascontiguousarray(words).view(ml_dtypes.float8_e4m3fn).astype(np.float64)
    else:
        nib = np.empty((g, p, n, 4), np.uint8)
        nib[..., 0::2] = words & 0xF
        nib[..., 1::2] = words >> 4
        vals = E2M1[nib]
    vals = vals * np.repeat(np.exp2(scales.astype(np.float64) - 127.0), 8, axis=1)[..., None]
    return vals.transpose(0, 1, 3, 2).reshape(g * 512, n)
def pack4(w):
    words, scales = pack_weight(w, "e2m1")
    return words.reshape(words.shape[0], 128, -1), scales


def unpack4(words, scales):
    return unpack_weight(words.reshape(words.shape[0], 128, -1, 2), scales, "e2m1")


M, KY, KU, J, F, N = 1024, 1536, 1024, 6, 256, 1536


def setup_inputs():
    s, t = mx_kscale(KY), mx_kscale(KU)
    w = np.random.standard_normal((KU, N)) / np.sqrt(KU) / t[:, None]
    w_words, w_scales = pack4(w)
    return {"y": bf(np.random.standard_normal((M, KY)) * s),
            "u": bf(np.random.standard_normal((M, KU)) * t),
            "v": bf(np.random.standard_normal((KY, N)) / np.sqrt(KY) / s[:, None]),
            "w_words": w_words,
            "w_scales": w_scales,
            "b": bf(0.3 * np.random.standard_normal(N)),
            "sig": bf(np.random.uniform(0.5, 1.5, (J, F)) / J)}


def reference(y, u, v, w_words, w_scales, b, sig):
    ry = mxq(f64(y), 1, "e4m3") @ mxq(f64(v), 0, "e4m3")
    ru = mxq(f64(u), 1, "e4m3") @ unpack4(w_words, w_scales)
    r = ry + ru + f64(b)
    e = np.square(r).reshape(M, J, F)
    return (e * f64(sig)).sum(axis=1)

@@ -1,0 +1,308 @@
+from contextlib import ExitStack
+
+import concourse.mybir as mybir
+from concourse.masks import make_identity
+
+F32 = mybir.dt.float32
+BF16 = mybir.dt.bfloat16
+U8 = mybir.dt.uint8
+U32 = mybir.dt.uint32
+I32 = mybir.dt.int32
+FP8X4 = mybir.dt.float8_e4m3fn_x4
+FP4X4 = mybir.dt.float4_e2m1fn_x4
+ALU = mybir.AluOpType
+ACT = mybir.ActivationFunctionType
+
+P = 128
+M, KY, KU, J, F = 1024, 1536, 1024, 6, 256
+N = J * F
+GY, GU = KY // 512, KU // 512
+FLOPS = 2 * M * N * (KY + KU)
+
+HALVES = 2
+MH = M // HALVES
+NT = N // P
+CHUNKS = 3
+CW = N // CHUNKS
+TPC = CW // P
+
+
+def tile_parity_fault_scores_s1_kernel(tc, y, u, v, w_words, w_scales, b, sig, out):
+    nc = tc.nc
+    with ExitStack() as ctx:
+        keep = ctx.enter_context(tc.tile_pool(name="keep", bufs=1))
+        vgp = ctx.enter_context(tc.tile_pool(name="vgroup", bufs=3))
+        epool = ctx.enter_context(tc.tile_pool(name="squares", bufs=8))
+        psum = ctx.enter_context(tc.psum_pool(name="psum", bufs=1))
+        ctx.enter_context(tc.manual_schedule())
+
+        def sb(shape, dtype, name):
+            return keep.tile(shape, dtype, name=name, align_bytes=64)
+
+        def bank(i):
+            return psum.tile([P, 512], F32, name=f"bank{i}", tag=f"bank{i}")
+
+        u_sb = [[sb([P, 2, KU], BF16, f"u_{h}_{q}") for q in range(2)] for h in range(HALVES)]
+        y_sb = [[sb([P, 2, KY], BF16, f"y_{h}_{q}") for q in range(2)] for h in range(HALVES)]
+        v_sb = [[sb([P, 4, CW], BF16, f"v_{c}_{g}") for g in range(GY)] for c in range(CHUNKS)]
+        w_sb = sb([P, GU, 2 * N], U8, "w_codes")
+        ws_sb = sb([P, GU, N], U8, "w_scale")
+        bsig = sb([P, P], BF16, "bsig")
+        bsig32 = sb([P, P], F32, "bsig32")
+        cols = sb([P, 2 * NT], F32, "cols")
+        ident = sb([P, P], F32, "ident")
+        warm = sb([P, 1], F32, "warm")
+
+        nc.vector.memset(ws_sb[:].rearrange("p g n -> p (g n)").bitcast(U32), 0)
+        make_identity(nc, ident[:])
+        nc.vector.memset(bsig[:], 0.0)
+        nc.vector.memset(warm[:], 0.0)
+        for q in range(4):
+            nc.gpsimd.dma_start(
+                out=ws_sb[32 * q : 32 * q + 4, :, :].bitcast(I32),
+                in_=w_scales[:, 4 * q : 4 * q + 4, :].rearrange("g q n -> q g n").bitcast(I32),
+            )
+        nc.gpsimd.dma_start(out=bsig[0:NT, :], in_=b.rearrange("(n f) -> n f", f=P))
+        nc.gpsimd.dma_start(out=bsig[NT : 2 * NT, :], in_=sig.rearrange("j (h f) -> (j h) f", f=P))
+        nc.scalar.activation(out=warm[:], in_=warm[:], func=ACT.Square)
+
+        def rows(x, h):
+            return x[h * MH : (h + 1) * MH, :].rearrange("(p i) k -> p i k", i=4)
+
+        def load_rows(dst, x, h, q, split):
+            if split:
+                for i in range(2):
+                    nc.sync.dma_start(out=dst[h][q][:, i, :], in_=rows(x, h)[:, 2 * q + i, :])
+            else:
+                nc.sync.dma_start(out=dst[h][q][:], in_=rows(x, h)[:, 2 * q : 2 * q + 2, :])
+
+        for h in range(HALVES):
+            for q in range(2):
+                load_rows(u_sb, u, h, q, h == 0 and q == 0)
+        nc.sync.dma_start(out=w_sb[:].bitcast(I32), in_=w_words.rearrange("g p n -> p g n").bitcast(I32))
+        for h in range(HALVES):
+            for q in range(2):
+                load_rows(y_sb, y, h, q, False)
+        for c in range(CHUNKS):
+            for g in range(GY):
+                nc.sync.dma_start(
+                    out=v_sb[c][g][:],
+                    in_=v[512 * g : 512 * (g + 1), c * CW : (c + 1) * CW].rearrange("(p j) c -> p j c", j=4),
+                )
+
+        ug = [sb([P, GU, 4 * MH], BF16, f"ug_{h}") for h in range(HALVES)]
+        yg = [sb([P, GY, 4 * MH], BF16, f"yg_{h}") for h in range(HALVES)]
+        uc = [sb([P, GU, MH], U32, f"uc_{h}") for h in range(HALVES)]
+        yc = [sb([P, GY, MH], U32, f"yc_{h}") for h in range(HALVES)]
+        us = [sb([P, GU, MH], U8, f"us_{h}") for h in range(HALVES)]
+        ys = [sb([P, GY, MH], U8, f"ys_{h}") for h in range(HALVES)]
+        vc = [[sb([P, CW], U32, f"vc_{c}_{g}") for g in range(GY)] for c in range(CHUNKS)]
+        vs = [[sb([P, CW], U8, f"vs_{c}_{g}") for g in range(GY)] for c in range(CHUNKS)]
+        acc = [[sb([P, MH], F32, f"acc_{h}_{f}") for f in range(2)] for h in range(HALVES)]
+        stage = [sb([P, 4, F], F32, f"stage_{h}") for h in range(HALVES)]
+
+        def transpose_pair(src, width, groups, banks):
+            words = src[:].rearrange("p i k -> p (i k)").bitcast(F32)
+            for i in range(2):
+                for n, g in enumerate(groups):
+                    for e in range(2):
+                        s = i * (width // 2) + 256 * g
+                        nc.tensor.transpose(
+                            banks[n][:, (2 * i + e) * P : (2 * i + e + 1) * P], words[:, s + e : s + 256 : 2], ident[:]
+                        )
+
+        def copy_unit(engine, bnk, dst, g, q):
+            o = dst[:, g, q * 1024 : (q + 1) * 1024].bitcast(F32).rearrange("p (i r e) -> p i r e", i=2, e=2)
+            x = bnk[:].rearrange("p (i e r) -> p i r e", i=2, e=2)
+            if engine == "v":
+                nc.vector.tensor_copy(out=o, in_=x)
+            else:
+                nc.scalar.copy(out=o, in_=x)
+
+        def quant_unit(codes, scales, src, g, q):
+            nc.vector.quantize_mx(
+                out=codes[:, g, q * 256 : (q + 1) * 256].bitcast(FP8X4),
+                scales=scales[:, g, q * 256 : (q + 1) * 256],
+                in_=src[:, g, q * 1024 : (q + 1) * 1024],
+            )
+
+        def copy_v(c, g, vcols, dst):
+            for engine, a, z in (("v", 0, vcols), ("s", vcols, CW)):
+                o = dst[:, 4 * a : 4 * z].rearrange("p (n t) -> p n t", t=4)
+                x = v_sb[c][g][:, :, a:z].rearrange("p t n -> p n t")
+                if engine == "v":
+                    nc.vector.tensor_copy(out=o, in_=x)
+                else:
+                    nc.scalar.copy(out=o, in_=x)
+
+        def quant_v(c, g, src):
+            nc.vector.quantize_mx(out=vc[c][g][:].bitcast(FP8X4), scales=vs[c][g][:], in_=src[:])
+
+        def mm_u(acc_bank, nt, h, g):
+            nc.tensor.matmul_mx(
+                out=acc_bank[:],
+                lhsT=w_sb[:, g, nt * 2 * P : (nt + 1) * 2 * P].bitcast(FP4X4),
+                lhsT_scale=ws_sb[:, g, nt * P : (nt + 1) * P],
+                rhs=uc[h][:, g, :].bitcast(FP8X4),
+                rhs_scale=us[h][:, g, :],
+                start=(g == 0),
+                stop=False,
+            )
+
+        def mm_y(acc_bank, nt, h, g):
+            c, t = divmod(nt, TPC)
+            nc.tensor.matmul_mx(
+                out=acc_bank[:],
+                lhsT=vc[c][g][:, t * P : (t + 1) * P].bitcast(FP8X4),
+                lhsT_scale=vs[c][g][:, t * P : (t + 1) * P],
+                rhs=yc[h][:, g, :].bitcast(FP8X4),
+                rhs_scale=ys[h][:, g, :],
+                start=False,
+                stop=(g == GY - 1),
+            )
+
+        pending = []
+
+        def flush(n):
+            while len(pending) > n:
+                pending.pop(0)()
+
+        open_banks = {}
+        unit = 0
+        rot = 0
+        for h in range(HALVES):
+            for q in range(2):
+                banks = [bank(4 + (rot + n) % 4) for n in range(GU)]
+                rot += GU
+                transpose_pair(u_sb[h][q], KU, range(GU), banks)
+                for g in range(GU):
+                    copy_unit("v" if unit % 5 in (1, 3) else "s", banks[g], ug[h], g, q)
+                    unit += 1
+                    pending.append(lambda h=h, g=g, q=q: quant_unit(uc[h], us[h], ug[h], g, q))
+                    flush(2)
+        for t in range(TPC):
+            open_banks[(t, 0)] = bank(t)
+            for g in range(GU):
+                mm_u(open_banks[(t, 0)], t, 0, g)
+        nc.vector.tensor_copy(out=bsig32[:], in_=bsig[:])
+        bt = bank(4 + rot % 4)
+        rot += 1
+        nc.tensor.transpose(bt[:, 0:P], bsig32[:], ident[:])
+        nc.scalar.copy(out=cols[:], in_=bt[:, 0 : 2 * NT])
+        for h in range(HALVES):
+            for q in range(2):
+                banks = [bank(4 + (rot + n) % 4) for n in range(GY)]
+                rot += GY
+                transpose_pair(y_sb[h][q], KY, range(GY), banks)
+                for g in range(GY):
+                    copy_unit("v" if unit % 5 in (1, 3) else "s", banks[g], yg[h], g, q)
+                    unit += 1
+                    pending.append(lambda h=h, g=g, q=q: quant_unit(yc[h], ys[h], yg[h], g, q))
+                    flush(2)
+        vg = {}
+
+        def new_vg(c, g):
+            vg[(c, g)] = vgp.tile([P, 4 * CW], BF16, name="vg", align_bytes=64)
+            return vg[(c, g)]
+
+        flush(0)
+        copy_v(0, 0, 320, new_vg(0, 0))
+        copy_v(0, 1, 320, new_vg(0, 1))
+        quant_v(0, 0, vg[(0, 0)])
+        copy_v(0, 2, 320, new_vg(0, 2))
+        quant_v(0, 1, vg[(0, 1)])
+        prep = []
+        for c in (1, 2):
+            for g in range(GY):
+                prep.append(lambda c=c, g=g: copy_v(c, g, 384, new_vg(c, g)))
+                if g > 0:
+                    prep.append(lambda c=c, g=g: quant_v(c, g - 1, vg[(c, g - 1)]))
+            prep.append(lambda c=c: quant_v(c, GY - 1, vg[(c, GY - 1)]))
+        for t in range(TPC):
+            open_banks[(t, 1)] = bank(4 + t)
+            for g in range(GU):
+                mm_u(open_banks[(t, 1)], t, 1, g)
+        prep.pop(0)()
+        quant_v(0, 2, vg[(0, 2)])
+
+        def square(nt, h, bnk, a=0, z=MH, e=None):
+            if e is None:
+                e = epool.tile([P, MH], F32, name="e", align_bytes=64)
+            nc.scalar.activation(out=e[:, a:z], in_=bnk[:, a:z], func=ACT.Square, bias=cols[:, nt : nt + 1])
+            return e
+
+        def weigh(nt, h, e, a=0, z=MH):
+            d = acc[h][nt % 2][:, a:z]
+            s = cols[:, NT + nt : NT + nt + 1]
+            if nt < 2:
+                nc.vector.tensor_scalar(out=d, in0=e[:, a:z], scalar1=s, scalar2=None, op0=ALU.mult)
+            else:
+                nc.vector.scalar_tensor_tensor(out=d, in0=e[:, a:z], scalar=s, in1=d, op0=ALU.mult, op1=ALU.add)
+
+        groups = [(t, h) for h in range(HALVES) for t in range(TPC)]
+        for t, h in groups:
+            mm_y(open_banks[(t, h)], t, h, 0)
+        for n, (t, h) in enumerate(groups):
+            for g in range(1, GY):
+                mm_y(open_banks[(t, h)], t, h, g)
+            e = square(t, h, open_banks[(t, h)])
+            pending.append(lambda t=t, h=h, e=e: weigh(t, h, e))
+            if n < 5:
+                prep.pop(0)()
+            flush(6)
+
+        def transposed(h, f, lo, hi, bnk):
+            for i in range(lo, hi):
+                nc.tensor.transpose(bnk[:, (i - lo) * P : (i - lo + 1) * P], acc[h][f][:, i * P : (i + 1) * P], ident[:])
+
+        def unload(engine, h, f, lo, hi, bnk):
+            o = stage[h][:, lo:hi, f * P : (f + 1) * P]
+            x = bnk[:, 0 : (hi - lo) * P].rearrange("p (i f) -> p i f", f=P)
+            if engine == "v":
+                nc.vector.tensor_copy(out=o, in_=x)
+            else:
+                nc.scalar.copy(out=o, in_=x)
+
+        def store(h, lo, hi):
+            nc.sync.dma_start(out=rows(out, h)[:, lo:hi, :], in_=stage[h][:, lo:hi, :])
+
+        lag = 6
+        for c in (1, 2):
+            for n, (t, h) in enumerate(groups):
+                nt = c * TPC + t
+                bnk = bank(4 * h + t)
+                for g in range(GU):
+                    mm_u(bnk, nt, h, g)
+                for g in range(GY):
+                    mm_y(bnk, nt, h, g)
+                if prep:
+                    prep.pop(0)()
+                if c == 2:
+                    lag = max(lag - 1, 0)
+                if (c, n) == (2, len(groups) - 1):
+                    flush(0)
+                    e = square(nt, h, bnk, 0, 256)
+                    square(nt, h, bnk, 256, 512, e)
+                    weigh(nt, h, e, 0, 256)
+                    weigh(nt, h, e, 256, 512)
+                else:
+                    e = square(nt, h, bnk)
+                    pending.append(lambda nt=nt, h=h, e=e: weigh(nt, h, e))
+                    flush(lag)
+                if (c, n) == (2, 6):
+                    for f in range(2):
+                        ob = bank(f)
+                        transposed(0, f, 0, 4, ob)
+                        unload("s", 0, f, 0, 4, ob)
+                    store(0, 0, 4)
+        b0 = bank(2)
+        transposed(1, 0, 0, 4, b0)
+        unload("s", 1, 0, 0, 4, b0)
+        b1 = bank(3)
+        transposed(1, 1, 0, 2, b1)
+        unload("v", 1, 1, 0, 2, b1)
+        store(1, 0, 2)
+        b2 = bank(0)
+        transposed(1, 1, 2, 4, b2)
+        unload("s", 1, 1, 2, 4, b2)
+        store(1, 2, 4)

@@ -23,6 +23,7 @@ HALVES = 2
 MH = M // HALVES
 NT = N // P
 CHUNKS = 3
+V_UNITS = (1, 3, 6, 9, 12, 15)
 CW = N // CHUNKS
 TPC = CW // P
 
@@ -57,11 +58,6 @@ def tile_parity_fault_scores_s1_kernel(tc, y, u, v, w_words, w_scales, b, sig, o
         make_identity(nc, ident[:])
         nc.vector.memset(bsig[:], 0.0)
         nc.vector.memset(warm[:], 0.0)
-        for q in range(4):
-            nc.gpsimd.dma_start(
-                out=ws_sb[32 * q : 32 * q + 4, :, :].bitcast(I32),
-                in_=w_scales[:, 4 * q : 4 * q + 4, :].rearrange("g q n -> q g n").bitcast(I32),
-            )
         nc.gpsimd.dma_start(out=bsig[0:NT, :], in_=b.rearrange("(n f) -> n f", f=P))
         nc.gpsimd.dma_start(out=bsig[NT : 2 * NT, :], in_=sig.rearrange("j (h f) -> (j h) f", f=P))
         nc.scalar.activation(out=warm[:], in_=warm[:], func=ACT.Square)
@@ -79,6 +75,12 @@ def tile_parity_fault_scores_s1_kernel(tc, y, u, v, w_words, w_scales, b, sig, o
         for h in range(HALVES):
             for q in range(2):
                 load_rows(u_sb, u, h, q, h == 0 and q == 0)
+                if h == 0 and q == 0:
+                    for s in range(4):
+                        nc.sync.dma_start(
+                            out=ws_sb[32 * s : 32 * s + 4, :, :].bitcast(I32),
+                            in_=w_scales[:, 4 * s : 4 * s + 4, :].rearrange("g q n -> q g n").bitcast(I32),
+                        )
         nc.sync.dma_start(out=w_sb[:].bitcast(I32), in_=w_words.rearrange("g p n -> p g n").bitcast(I32))
         for h in range(HALVES):
             for q in range(2):
@@ -101,15 +103,17 @@ def tile_parity_fault_scores_s1_kernel(tc, y, u, v, w_words, w_scales, b, sig, o
         acc = [[sb([P, MH], F32, f"acc_{h}_{f}") for f in range(2)] for h in range(HALVES)]
         stage = [sb([P, 4, F], F32, f"stage_{h}") for h in range(HALVES)]
 
-        def transpose_pair(src, width, groups, banks):
+        def transpose_pair(src, width, groups, banks, rows_first=False):
             words = src[:].rearrange("p i k -> p (i k)").bitcast(F32)
-            for i in range(2):
-                for n, g in enumerate(groups):
-                    for e in range(2):
-                        s = i * (width // 2) + 256 * g
-                        nc.tensor.transpose(
-                            banks[n][:, (2 * i + e) * P : (2 * i + e + 1) * P], words[:, s + e : s + 256 : 2], ident[:]
-                        )
+            steps = [(i, g) for g in groups for i in range(2)]
+            if rows_first:
+                steps = [(i, g) for i in range(2) for g in groups]
+            for i, g in steps:
+                for e in range(2):
+                    s = i * (width // 2) + 256 * g
+                    nc.tensor.transpose(
+                        banks[g][:, (2 * i + e) * P : (2 * i + e + 1) * P], words[:, s + e : s + 256 : 2], ident[:]
+                    )
 
         def copy_unit(engine, bnk, dst, g, q):
             o = dst[:, g, q * 1024 : (q + 1) * 1024].bitcast(F32).rearrange("p (i r e) -> p i r e", i=2, e=2)
@@ -138,25 +142,25 @@ def tile_parity_fault_scores_s1_kernel(tc, y, u, v, w_words, w_scales, b, sig, o
         def quant_v(c, g, src):
             nc.vector.quantize_mx(out=vc[c][g][:].bitcast(FP8X4), scales=vs[c][g][:], in_=src[:])
 
-        def mm_u(acc_bank, nt, h, g):
+        def mm_u(acc_bank, nt, h, g, win=slice(0, MH)):
             nc.tensor.matmul_mx(
-                out=acc_bank[:],
+                out=acc_bank[:, 0 : win.stop - win.start],
                 lhsT=w_sb[:, g, nt * 2 * P : (nt + 1) * 2 * P].bitcast(FP4X4),
                 lhsT_scale=ws_sb[:, g, nt * P : (nt + 1) * P],
-                rhs=uc[h][:, g, :].bitcast(FP8X4),
-                rhs_scale=us[h][:, g, :],
+                rhs=uc[h][:, g, win].bitcast(FP8X4),
+                rhs_scale=us[h][:, g, win],
                 start=(g == 0),
                 stop=False,
             )
 
-        def mm_y(acc_bank, nt, h, g):
+        def mm_y(acc_bank, nt, h, g, win=slice(0, MH)):
             c, t = divmod(nt, TPC)
             nc.tensor.matmul_mx(
-                out=acc_bank[:],
+                out=acc_bank[:, 0 : win.stop - win.start],
                 lhsT=vc[c][g][:, t * P : (t + 1) * P].bitcast(FP8X4),
                 lhsT_scale=vs[c][g][:, t * P : (t + 1) * P],
-                rhs=yc[h][:, g, :].bitcast(FP8X4),
-                rhs_scale=ys[h][:, g, :],
+                rhs=yc[h][:, g, win].bitcast(FP8X4),
+                rhs_scale=ys[h][:, g, win],
                 start=False,
                 stop=(g == GY - 1),
             )
@@ -167,6 +171,9 @@ def tile_parity_fault_scores_s1_kernel(tc, y, u, v, w_words, w_scales, b, sig, o
             while len(pending) > n:
                 pending.pop(0)()
 
+        def hbank(t, h):
+            return t if h == 0 else 4 + (t + 1) % 4
+
         open_banks = {}
         unit = 0
         rot = 0
@@ -174,9 +181,9 @@ def tile_parity_fault_scores_s1_kernel(tc, y, u, v, w_words, w_scales, b, sig, o
             for q in range(2):
                 banks = [bank(4 + (rot + n) % 4) for n in range(GU)]
                 rot += GU
-                transpose_pair(u_sb[h][q], KU, range(GU), banks)
+                transpose_pair(u_sb[h][q], KU, range(GU), banks, h == 0 and q == 0)
                 for g in range(GU):
-                    copy_unit("v" if unit % 5 in (1, 3) else "s", banks[g], ug[h], g, q)
+                    copy_unit("v" if unit in V_UNITS else "s", banks[g], ug[h], g, q)
                     unit += 1
                     pending.append(lambda h=h, g=g, q=q: quant_unit(uc[h], us[h], ug[h], g, q))
                     flush(2)
@@ -195,7 +202,7 @@ def tile_parity_fault_scores_s1_kernel(tc, y, u, v, w_words, w_scales, b, sig, o
                 rot += GY
                 transpose_pair(y_sb[h][q], KY, range(GY), banks)
                 for g in range(GY):
-                    copy_unit("v" if unit % 5 in (1, 3) else "s", banks[g], yg[h], g, q)
+                    copy_unit("v" if unit in V_UNITS else "s", banks[g], yg[h], g, q)
                     unit += 1
                     pending.append(lambda h=h, g=g, q=q: quant_unit(yc[h], ys[h], yg[h], g, q))
                     flush(2)
@@ -205,25 +212,25 @@ def tile_parity_fault_scores_s1_kernel(tc, y, u, v, w_words, w_scales, b, sig, o
             vg[(c, g)] = vgp.tile([P, 4 * CW], BF16, name="vg", align_bytes=64)
             return vg[(c, g)]
 
+        copy_v(0, 0, 288, new_vg(0, 0))
         flush(0)
-        copy_v(0, 0, 320, new_vg(0, 0))
-        copy_v(0, 1, 320, new_vg(0, 1))
         quant_v(0, 0, vg[(0, 0)])
-        copy_v(0, 2, 320, new_vg(0, 2))
+        copy_v(0, 1, 256, new_vg(0, 1))
+        copy_v(0, 2, 256, new_vg(0, 2))
         quant_v(0, 1, vg[(0, 1)])
         prep = []
         for c in (1, 2):
             for g in range(GY):
-                prep.append(lambda c=c, g=g: copy_v(c, g, 384, new_vg(c, g)))
+                prep.append(lambda c=c, g=g: copy_v(c, g, 256 if (c, g) == (1, 0) else 384, new_vg(c, g)))
                 if g > 0:
                     prep.append(lambda c=c, g=g: quant_v(c, g - 1, vg[(c, g - 1)]))
             prep.append(lambda c=c: quant_v(c, GY - 1, vg[(c, GY - 1)]))
         for t in range(TPC):
-            open_banks[(t, 1)] = bank(4 + t)
+            open_banks[(t, 1)] = bank(hbank(t, 1))
             for g in range(GU):
                 mm_u(open_banks[(t, 1)], t, 1, g)
-        prep.pop(0)()
         quant_v(0, 2, vg[(0, 2)])
+        prep.pop(0)()
 
         def square(nt, h, bnk, a=0, z=MH, e=None):
             if e is None:
@@ -267,10 +274,13 @@ def tile_parity_fault_scores_s1_kernel(tc, y, u, v, w_words, w_scales, b, sig, o
             nc.sync.dma_start(out=rows(out, h)[:, lo:hi, :], in_=stage[h][:, lo:hi, :])
 
         lag = 6
+        order = [(t, 0) for t in range(TPC)] + [(t, 1) for t in (0, 2, 1, 3)]
         for c in (1, 2):
-            for n, (t, h) in enumerate(groups):
+            for n, (t, h) in enumerate(order):
+                if (c, n) == (2, len(order) - 1):
+                    break
                 nt = c * TPC + t
-                bnk = bank(4 * h + t)
+                bnk = bank(hbank(t, h))
                 for g in range(GU):
                     mm_u(bnk, nt, h, g)
                 for g in range(GY):
@@ -278,31 +288,34 @@ def tile_parity_fault_scores_s1_kernel(tc, y, u, v, w_words, w_scales, b, sig, o
                 if prep:
                     prep.pop(0)()
                 if c == 2:
-                    lag = max(lag - 1, 0)
-                if (c, n) == (2, len(groups) - 1):
-                    flush(0)
-                    e = square(nt, h, bnk, 0, 256)
-                    square(nt, h, bnk, 256, 512, e)
-                    weigh(nt, h, e, 0, 256)
-                    weigh(nt, h, e, 256, 512)
-                else:
-                    e = square(nt, h, bnk)
-                    pending.append(lambda nt=nt, h=h, e=e: weigh(nt, h, e))
-                    flush(lag)
-                if (c, n) == (2, 6):
-                    for f in range(2):
-                        ob = bank(f)
-                        transposed(0, f, 0, 4, ob)
-                        unload("s", 0, f, 0, 4, ob)
+                    lag = max(lag - 2, 0)
+                e = square(nt, h, bnk)
+                pending.append(lambda nt=nt, h=h, e=e: weigh(nt, h, e))
+                flush(lag)
+                if (c, n) == (2, 5):
+                    for f, engine in ((0, "s"), (1, "v")):
+                        obk = bank(f)
+                        transposed(0, f, 0, 4, obk)
+                        unload(engine, 0, f, 0, 4, obk)
                     store(0, 0, 4)
-        b0 = bank(2)
-        transposed(1, 0, 0, 4, b0)
-        unload("s", 1, 0, 0, 4, b0)
-        b1 = bank(3)
-        transposed(1, 1, 0, 2, b1)
-        unload("v", 1, 1, 0, 2, b1)
-        store(1, 0, 2)
-        b2 = bank(0)
-        transposed(1, 1, 2, 4, b2)
-        unload("s", 1, 1, 2, 4, b2)
-        store(1, 2, 4)
+        nt, h = NT - 1, 1
+        quarter = [bank(i) for i in (2, 3, 0, hbank(3, 1))]
+        e = epool.tile([P, MH], F32, name="e", align_bytes=64)
+        for i in range(4):
+            if i == 1:
+                obk = bank(1)
+                transposed(1, 0, 0, 4, obk)
+                unload("s", 1, 0, 0, 4, obk)
+            win = slice(i * P, (i + 1) * P)
+            bq = quarter[i]
+            for g in range(GU):
+                mm_u(bq, nt, h, g, win)
+            for g in range(GY):
+                mm_y(bq, nt, h, g, win)
+            nc.scalar.activation(out=e[:, win], in_=bq[:, 0:P], func=ACT.Square, bias=cols[:, nt : nt + 1])
+            weigh(nt, h, e, i * P, (i + 1) * P)
+        for half, engine in ((0, "s"), (1, "v")):
+            obk = bank((hbank(0, 1), hbank(2, 1))[half])
+            transposed(1, 1, 2 * half, 2 * half + 2, obk)
+            unload(engine, 1, 1, 2 * half, 2 * half + 2, obk)
+            store(1, 2 * half, 2 * half + 2)

@@ -46,7 +46,7 @@ def tile_parity_fault_scores_s1_kernel(tc, y, u, v, w_words, w_scales, b, sig, o
         u_sb = [[sb([P, 2, KU], BF16, f"u_{h}_{q}") for q in range(2)] for h in range(HALVES)]
         y_sb = [[sb([P, 2, KY], BF16, f"y_{h}_{q}") for q in range(2)] for h in range(HALVES)]
         v_sb = [[sb([P, 4, CW], BF16, f"v_{c}_{g}") for g in range(GY)] for c in range(CHUNKS)]
-        w_sb = sb([P, GU, 2 * N], U8, "w_codes")
+        w_sb = [sb([P, GU, 2 * CW], U8, f"w_{c}") for c in range(CHUNKS)]
         ws_sb = sb([P, GU, N], U8, "w_scale")
         bsig = sb([P, P], BF16, "bsig")
         bsig32 = sb([P, P], F32, "bsig32")
@@ -58,8 +58,8 @@ def tile_parity_fault_scores_s1_kernel(tc, y, u, v, w_words, w_scales, b, sig, o
         make_identity(nc, ident[:])
         nc.vector.memset(bsig[:], 0.0)
         nc.vector.memset(warm[:], 0.0)
-        nc.gpsimd.dma_start(out=bsig[0:NT, :], in_=b.rearrange("(n f) -> n f", f=P))
-        nc.gpsimd.dma_start(out=bsig[NT : 2 * NT, :], in_=sig.rearrange("j (h f) -> (j h) f", f=P))
+        nc.scalar.dma_start(out=bsig[0:NT, :], in_=b.rearrange("(n f) -> n f", f=P))
+        nc.scalar.dma_start(out=bsig[NT : 2 * NT, :], in_=sig.rearrange("j (h f) -> (j h) f", f=P))
         nc.scalar.activation(out=warm[:], in_=warm[:], func=ACT.Square)
 
         def rows(x, h):
@@ -72,20 +72,29 @@ def tile_parity_fault_scores_s1_kernel(tc, y, u, v, w_words, w_scales, b, sig, o
             else:
                 nc.sync.dma_start(out=dst[h][q][:], in_=rows(x, h)[:, 2 * q : 2 * q + 2, :])
 
+        def load_w(c):
+            nc.sync.dma_start(
+                out=w_sb[c][:].bitcast(I32),
+                in_=w_words[:, :, 2 * c * CW : 2 * (c + 1) * CW].rearrange("g p n -> p g n").bitcast(I32),
+            )
+
         for h in range(HALVES):
             for q in range(2):
                 load_rows(u_sb, u, h, q, h == 0 and q == 0)
-                if h == 0 and q == 0:
+                if h == 0 and q == 1:
                     for s in range(4):
                         nc.sync.dma_start(
                             out=ws_sb[32 * s : 32 * s + 4, :, :].bitcast(I32),
                             in_=w_scales[:, 4 * s : 4 * s + 4, :].rearrange("g q n -> q g n").bitcast(I32),
                         )
-        nc.sync.dma_start(out=w_sb[:].bitcast(I32), in_=w_words.rearrange("g p n -> p g n").bitcast(I32))
+                if h == 1 and q == 0:
+                    load_w(0)
         for h in range(HALVES):
             for q in range(2):
                 load_rows(y_sb, y, h, q, False)
         for c in range(CHUNKS):
+            if c > 0:
+                load_w(c)
             for g in range(GY):
                 nc.sync.dma_start(
                     out=v_sb[c][g][:],
@@ -132,8 +141,8 @@ def tile_parity_fault_scores_s1_kernel(tc, y, u, v, w_words, w_scales, b, sig, o
 
         def copy_v(c, g, vcols, dst):
             for engine, a, z in (("v", 0, vcols), ("s", vcols, CW)):
-                o = dst[:, 4 * a : 4 * z].rearrange("p (n t) -> p n t", t=4)
-                x = v_sb[c][g][:, :, a:z].rearrange("p t n -> p n t")
+                o = dst[:, 4 * a : 4 * z].rearrange("p (n i t) -> p n t i", i=4, t=4)
+                x = v_sb[c][g][:, :, a:z].rearrange("p t (n i) -> p n t i", i=4)
                 if engine == "v":
                     nc.vector.tensor_copy(out=o, in_=x)
                 else:
@@ -145,7 +154,7 @@ def tile_parity_fault_scores_s1_kernel(tc, y, u, v, w_words, w_scales, b, sig, o
         def mm_u(acc_bank, nt, h, g, win=slice(0, MH)):
             nc.tensor.matmul_mx(
                 out=acc_bank[:, 0 : win.stop - win.start],
-                lhsT=w_sb[:, g, nt * 2 * P : (nt + 1) * 2 * P].bitcast(FP4X4),
+                lhsT=w_sb[nt // TPC][:, g, (nt % TPC) * 2 * P : (nt % TPC + 1) * 2 * P].bitcast(FP4X4),
                 lhsT_scale=ws_sb[:, g, nt * P : (nt + 1) * P],
                 rhs=uc[h][:, g, win].bitcast(FP8X4),
                 rhs_scale=us[h][:, g, win],
@@ -179,6 +188,13 @@ def tile_parity_fault_scores_s1_kernel(tc, y, u, v, w_words, w_scales, b, sig, o
         rot = 0
         for h in range(HALVES):
             for q in range(2):
+                if (h, q) == (1, 1):
+                    flush(0)
+                    nc.vector.tensor_copy(out=bsig32[:], in_=bsig[:])
+                    for t in range(TPC):
+                        open_banks[(t, 0)] = bank(t)
+                        for g in range(GU):
+                            mm_u(open_banks[(t, 0)], t, 0, g)
                 banks = [bank(4 + (rot + n) % 4) for n in range(GU)]
                 rot += GU
                 transpose_pair(u_sb[h][q], KU, range(GU), banks, h == 0 and q == 0)
@@ -187,11 +203,6 @@ def tile_parity_fault_scores_s1_kernel(tc, y, u, v, w_words, w_scales, b, sig, o
                     unit += 1
                     pending.append(lambda h=h, g=g, q=q: quant_unit(uc[h], us[h], ug[h], g, q))
                     flush(2)
-        for t in range(TPC):
-            open_banks[(t, 0)] = bank(t)
-            for g in range(GU):
-                mm_u(open_banks[(t, 0)], t, 0, g)
-        nc.vector.tensor_copy(out=bsig32[:], in_=bsig[:])
         bt = bank(4 + rot % 4)
         rot += 1
         nc.tensor.transpose(bt[:, 0:P], bsig32[:], ident[:])
@@ -212,7 +223,7 @@ def tile_parity_fault_scores_s1_kernel(tc, y, u, v, w_words, w_scales, b, sig, o
             vg[(c, g)] = vgp.tile([P, 4 * CW], BF16, name="vg", align_bytes=64)
             return vg[(c, g)]
 
-        copy_v(0, 0, 288, new_vg(0, 0))
+        copy_v(0, 0, 384, new_vg(0, 0))
         flush(0)
         quant_v(0, 0, vg[(0, 0)])
         copy_v(0, 1, 256, new_vg(0, 1))

from contextlib import ExitStack

import concourse.mybir as mybir
from concourse.masks import make_identity

F32 = mybir.dt.float32
BF16 = mybir.dt.bfloat16
U8 = mybir.dt.uint8
U32 = mybir.dt.uint32
I32 = mybir.dt.int32
FP8X4 = mybir.dt.float8_e4m3fn_x4
FP4X4 = mybir.dt.float4_e2m1fn_x4
ALU = mybir.AluOpType
ACT = mybir.ActivationFunctionType

P = 128
M, KY, KU, J, F = 1024, 1536, 1024, 6, 256
N = J * F
GY, GU = KY // 512, KU // 512
FLOPS = 2 * M * N * (KY + KU)

HALVES = 2
MH = M // HALVES
NT = N // P
CHUNKS = 3
V_UNITS = (1, 3, 6, 9, 12, 15)
CW = N // CHUNKS
TPC = CW // P


def tile_parity_fault_scores_s1_kernel(tc, y, u, v, w_words, w_scales, b, sig, out):
    nc = tc.nc
    with ExitStack() as ctx:
        keep = ctx.enter_context(tc.tile_pool(name="keep", bufs=1))
        vgp = ctx.enter_context(tc.tile_pool(name="vgroup", bufs=3))
        epool = ctx.enter_context(tc.tile_pool(name="squares", bufs=8))
        psum = ctx.enter_context(tc.psum_pool(name="psum", bufs=1))
        ctx.enter_context(tc.manual_schedule())

        def sb(shape, dtype, name):
            return keep.tile(shape, dtype, name=name, align_bytes=64)

        def bank(i):
            return psum.tile([P, 512], F32, name=f"bank{i}", tag=f"bank{i}")

        u_sb = [[sb([P, 2, KU], BF16, f"u_{h}_{q}") for q in range(2)] for h in range(HALVES)]
        y_sb = [[sb([P, 2, KY], BF16, f"y_{h}_{q}") for q in range(2)] for h in range(HALVES)]
        v_sb = [[sb([P, 4, CW], BF16, f"v_{c}_{g}") for g in range(GY)] for c in range(CHUNKS)]
        w_sb = [sb([P, GU, 2 * CW], U8, f"w_{c}") for c in range(CHUNKS)]
        ws_sb = sb([P, GU, N], U8, "w_scale")
        bsig = sb([P, P], BF16, "bsig")
        bsig32 = sb([P, P], F32, "bsig32")
        cols = sb([P, 2 * NT], F32, "cols")
        ident = sb([P, P], F32, "ident")
        warm = sb([P, 1], F32, "warm")

        nc.vector.memset(ws_sb[:].rearrange("p g n -> p (g n)").bitcast(U32), 0)
        make_identity(nc, ident[:])
        nc.vector.memset(bsig[:], 0.0)
        nc.vector.memset(warm[:], 0.0)
        nc.scalar.dma_start(out=bsig[0:NT, :], in_=b.rearrange("(n f) -> n f", f=P))
        nc.scalar.dma_start(out=bsig[NT : 2 * NT, :], in_=sig.rearrange("j (h f) -> (j h) f", f=P))
        nc.scalar.activation(out=warm[:], in_=warm[:], func=ACT.Square)

        def rows(x, h):
            return x[h * MH : (h + 1) * MH, :].rearrange("(p i) k -> p i k", i=4)

        def load_rows(dst, x, h, q, split):
            if split:
                for i in range(2):
                    nc.sync.dma_start(out=dst[h][q][:, i, :], in_=rows(x, h)[:, 2 * q + i, :])
            else:
                nc.sync.dma_start(out=dst[h][q][:], in_=rows(x, h)[:, 2 * q : 2 * q + 2, :])

        def load_w(c):
            nc.sync.dma_start(
                out=w_sb[c][:].bitcast(I32),
                in_=w_words[:, :, 2 * c * CW : 2 * (c + 1) * CW].rearrange("g p n -> p g n").bitcast(I32),
            )

        for h in range(HALVES):
            for q in range(2):
                load_rows(u_sb, u, h, q, h == 0 and q == 0)
                if h == 0 and q == 1:
                    for s in range(4):
                        nc.sync.dma_start(
                            out=ws_sb[32 * s : 32 * s + 4, :, :].bitcast(I32),
                            in_=w_scales[:, 4 * s : 4 * s + 4, :].rearrange("g q n -> q g n").bitcast(I32),
                        )
                if h == 1 and q == 0:
                    load_w(0)
        for h in range(HALVES):
            for q in range(2):
                load_rows(y_sb, y, h, q, False)
        for c in range(CHUNKS):
            if c > 0:
                load_w(c)
            for g in range(GY):
                nc.sync.dma_start(
                    out=v_sb[c][g][:],
                    in_=v[512 * g : 512 * (g + 1), c * CW : (c + 1) * CW].rearrange("(p j) c -> p j c", j=4),
                )

        ug = [sb([P, GU, 4 * MH], BF16, f"ug_{h}") for h in range(HALVES)]
        yg = [sb([P, GY, 4 * MH], BF16, f"yg_{h}") for h in range(HALVES)]
        uc = [sb([P, GU, MH], U32, f"uc_{h}") for h in range(HALVES)]
        yc = [sb([P, GY, MH], U32, f"yc_{h}") for h in range(HALVES)]
        us = [sb([P, GU, MH], U8, f"us_{h}") for h in range(HALVES)]
        ys = [sb([P, GY, MH], U8, f"ys_{h}") for h in range(HALVES)]
        vc = [[sb([P, CW], U32, f"vc_{c}_{g}") for g in range(GY)] for c in range(CHUNKS)]
        vs = [[sb([P, CW], U8, f"vs_{c}_{g}") for g in range(GY)] for c in range(CHUNKS)]
        acc = [[sb([P, MH], F32, f"acc_{h}_{f}") for f in range(2)] for h in range(HALVES)]
        stage = [sb([P, 4, F], F32, f"stage_{h}") for h in range(HALVES)]

        def transpose_pair(src, width, groups, banks, rows_first=False):
            words = src[:].rearrange("p i k -> p (i k)").bitcast(F32)
            steps = [(i, g) for g in groups for i in range(2)]
            if rows_first:
                steps = [(i, g) for i in range(2) for g in groups]
            for i, g in steps:
                for e in range(2):
                    s = i * (width // 2) + 256 * g
                    nc.tensor.transpose(
                        banks[g][:, (2 * i + e) * P : (2 * i + e + 1) * P], words[:, s + e : s + 256 : 2], ident[:]
                    )

        def copy_unit(engine, bnk, dst, g, q):
            o = dst[:, g, q * 1024 : (q + 1) * 1024].bitcast(F32).rearrange("p (i r e) -> p i r e", i=2, e=2)
            x = bnk[:].rearrange("p (i e r) -> p i r e", i=2, e=2)
            if engine == "v":
                nc.vector.tensor_copy(out=o, in_=x)
            else:
                nc.scalar.copy(out=o, in_=x)

        def quant_unit(codes, scales, src, g, q):
            nc.vector.quantize_mx(
                out=codes[:, g, q * 256 : (q + 1) * 256].bitcast(FP8X4),
                scales=scales[:, g, q * 256 : (q + 1) * 256],
                in_=src[:, g, q * 1024 : (q + 1) * 1024],
            )

        def copy_v(c, g, vcols, dst):
            for engine, a, z in (("v", 0, vcols), ("s", vcols, CW)):
                o = dst[:, 4 * a : 4 * z].rearrange("p (n i t) -> p n t i", i=4, t=4)
                x = v_sb[c][g][:, :, a:z].rearrange("p t (n i) -> p n t i", i=4)
                if engine == "v":
                    nc.vector.tensor_copy(out=o, in_=x)
                else:
                    nc.scalar.copy(out=o, in_=x)

        def quant_v(c, g, src):
            nc.vector.quantize_mx(out=vc[c][g][:].bitcast(FP8X4), scales=vs[c][g][:], in_=src[:])

        def mm_u(acc_bank, nt, h, g, win=slice(0, MH)):
            nc.tensor.matmul_mx(
                out=acc_bank[:, 0 : win.stop - win.start],
                lhsT=w_sb[nt // TPC][:, g, (nt % TPC) * 2 * P : (nt % TPC + 1) * 2 * P].bitcast(FP4X4),
                lhsT_scale=ws_sb[:, g, nt * P : (nt + 1) * P],
                rhs=uc[h][:, g, win].bitcast(FP8X4),
                rhs_scale=us[h][:, g, win],
                start=(g == 0),
                stop=False,
            )

        def mm_y(acc_bank, nt, h, g, win=slice(0, MH)):
            c, t = divmod(nt, TPC)
            nc.tensor.matmul_mx(
                out=acc_bank[:, 0 : win.stop - win.start],
                lhsT=vc[c][g][:, t * P : (t + 1) * P].bitcast(FP8X4),
                lhsT_scale=vs[c][g][:, t * P : (t + 1) * P],
                rhs=yc[h][:, g, win].bitcast(FP8X4),
                rhs_scale=ys[h][:, g, win],
                start=False,
                stop=(g == GY - 1),
            )

        pending = []

        def flush(n):
            while len(pending) > n:
                pending.pop(0)()

        def hbank(t, h):
            return t if h == 0 else 4 + (t + 1) % 4

        open_banks = {}
        unit = 0
        rot = 0
        for h in range(HALVES):
            for q in range(2):
                if (h, q) == (1, 1):
                    flush(0)
                    nc.vector.tensor_copy(out=bsig32[:], in_=bsig[:])
                    for t in range(TPC):
                        open_banks[(t, 0)] = bank(t)
                        for g in range(GU):
                            mm_u(open_banks[(t, 0)], t, 0, g)
                banks = [bank(4 + (rot + n) % 4) for n in range(GU)]
                rot += GU
                transpose_pair(u_sb[h][q], KU, range(GU), banks, h == 0 and q == 0)
                for g in range(GU):
                    copy_unit("v" if unit in V_UNITS else "s", banks[g], ug[h], g, q)
                    unit += 1
                    pending.append(lambda h=h, g=g, q=q: quant_unit(uc[h], us[h], ug[h], g, q))
                    flush(2)
        bt = bank(4 + rot % 4)
        rot += 1
        nc.tensor.transpose(bt[:, 0:P], bsig32[:], ident[:])
        nc.scalar.copy(out=cols[:], in_=bt[:, 0 : 2 * NT])
        for h in range(HALVES):
            for q in range(2):
                banks = [bank(4 + (rot + n) % 4) for n in range(GY)]
                rot += GY
                transpose_pair(y_sb[h][q], KY, range(GY), banks)
                for g in range(GY):
                    copy_unit("v" if unit in V_UNITS else "s", banks[g], yg[h], g, q)
                    unit += 1
                    pending.append(lambda h=h, g=g, q=q: quant_unit(yc[h], ys[h], yg[h], g, q))
                    flush(2)
        vg = {}

        def new_vg(c, g):
            vg[(c, g)] = vgp.tile([P, 4 * CW], BF16, name="vg", align_bytes=64)
            return vg[(c, g)]

        copy_v(0, 0, 384, new_vg(0, 0))
        flush(0)
        quant_v(0, 0, vg[(0, 0)])
        copy_v(0, 1, 256, new_vg(0, 1))
        copy_v(0, 2, 256, new_vg(0, 2))
        quant_v(0, 1, vg[(0, 1)])
        prep = []
        for c in (1, 2):
            for g in range(GY):
                prep.append(lambda c=c, g=g: copy_v(c, g, 256 if (c, g) == (1, 0) else 384, new_vg(c, g)))
                if g > 0:
                    prep.append(lambda c=c, g=g: quant_v(c, g - 1, vg[(c, g - 1)]))
            prep.append(lambda c=c: quant_v(c, GY - 1, vg[(c, GY - 1)]))
        for t in range(TPC):
            open_banks[(t, 1)] = bank(hbank(t, 1))
            for g in range(GU):
                mm_u(open_banks[(t, 1)], t, 1, g)
        quant_v(0, 2, vg[(0, 2)])
        prep.pop(0)()

        def square(nt, h, bnk, a=0, z=MH, e=None):
            if e is None:
                e = epool.tile([P, MH], F32, name="e", align_bytes=64)
            nc.scalar.activation(out=e[:, a:z], in_=bnk[:, a:z], func=ACT.Square, bias=cols[:, nt : nt + 1])
            return e

        def weigh(nt, h, e, a=0, z=MH):
            d = acc[h][nt % 2][:, a:z]
            s = cols[:, NT + nt : NT + nt + 1]
            if nt < 2:
                nc.vector.tensor_scalar(out=d, in0=e[:, a:z], scalar1=s, scalar2=None, op0=ALU.mult)
            else:
                nc.vector.scalar_tensor_tensor(out=d, in0=e[:, a:z], scalar=s, in1=d, op0=ALU.mult, op1=ALU.add)

        groups = [(t, h) for h in range(HALVES) for t in range(TPC)]
        for t, h in groups:
            mm_y(open_banks[(t, h)], t, h, 0)
        for n, (t, h) in enumerate(groups):
            for g in range(1, GY):
                mm_y(open_banks[(t, h)], t, h, g)
            e = square(t, h, open_banks[(t, h)])
            pending.append(lambda t=t, h=h, e=e: weigh(t, h, e))
            if n < 5:
                prep.pop(0)()
            flush(6)

        def transposed(h, f, lo, hi, bnk):
            for i in range(lo, hi):
                nc.tensor.transpose(bnk[:, (i - lo) * P : (i - lo + 1) * P], acc[h][f][:, i * P : (i + 1) * P], ident[:])

        def unload(engine, h, f, lo, hi, bnk):
            o = stage[h][:, lo:hi, f * P : (f + 1) * P]
            x = bnk[:, 0 : (hi - lo) * P].rearrange("p (i f) -> p i f", f=P)
            if engine == "v":
                nc.vector.tensor_copy(out=o, in_=x)
            else:
                nc.scalar.copy(out=o, in_=x)

        def store(h, lo, hi):
            nc.sync.dma_start(out=rows(out, h)[:, lo:hi, :], in_=stage[h][:, lo:hi, :])

        lag = 6
        order = [(t, 0) for t in range(TPC)] + [(t, 1) for t in (0, 2, 1, 3)]
        for c in (1, 2):
            for n, (t, h) in enumerate(order):
                if (c, n) == (2, len(order) - 1):
                    break
                nt = c * TPC + t
                bnk = bank(hbank(t, h))
                for g in range(GU):
                    mm_u(bnk, nt, h, g)
                for g in range(GY):
                    mm_y(bnk, nt, h, g)
                if prep:
                    prep.pop(0)()
                if c == 2:
                    lag = max(lag - 2, 0)
                e = square(nt, h, bnk)
                pending.append(lambda nt=nt, h=h, e=e: weigh(nt, h, e))
                flush(lag)
                if (c, n) == (2, 5):
                    for f, engine in ((0, "s"), (1, "v")):
                        obk = bank(f)
                        transposed(0, f, 0, 4, obk)
                        unload(engine, 0, f, 0, 4, obk)
                    store(0, 0, 4)
        nt, h = NT - 1, 1
        quarter = [bank(i) for i in (2, 3, 0, hbank(3, 1))]
        e = epool.tile([P, MH], F32, name="e", align_bytes=64)
        for i in range(4):
            if i == 1:
                obk = bank(1)
                transposed(1, 0, 0, 4, obk)
                unload("s", 1, 0, 0, 4, obk)
            win = slice(i * P, (i + 1) * P)
            bq = quarter[i]
            for g in range(GU):
                mm_u(bq, nt, h, g, win)
            for g in range(GY):
                mm_y(bq, nt, h, g, win)
            nc.scalar.activation(out=e[:, win], in_=bq[:, 0:P], func=ACT.Square, bias=cols[:, nt : nt + 1])
            weigh(nt, h, e, i * P, (i + 1) * P)
        for half, engine in ((0, "s"), (1, "v")):
            obk = bank((hbank(0, 1), hbank(2, 1))[half])
            transposed(1, 1, 2 * half, 2 * half + 2, obk)
            unload(engine, 1, 1, 2 * half, 2 * half + 2, obk)
            store(1, 2 * half, 2 * half + 2)
